import numpy as np
import ml_dtypes


def mxq(x, axis, fmt="e4m3"):
    dtype, down = {"e4m3": (ml_dtypes.float8_e4m3fn, 7), "e5m2": (ml_dtypes.float8_e5m2, 14)}[fmt]
    v = np.moveaxis(np.asarray(x, np.float32).astype(ml_dtypes.bfloat16).astype(np.float64), axis, -1)
    blocks = v.reshape(v.shape[:-1] + (-1, 32))
    amax = np.abs(blocks).max(-1, keepdims=True)
    byte = np.maximum(np.where(amax > 0, np.frexp(amax)[1] - 1 + 127, 0) - down, 1)
    scale = np.exp2(byte - 127.0)
    codes = (blocks / scale).astype(np.float32).astype(dtype).astype(np.float64)
    return np.moveaxis((codes * scale).reshape(v.shape), -1, axis)


WIDE = False


def mx_kscale(k):
    if not WIDE:
        return np.ones(k)
    levels = np.array([30, -30])
    if k % 512:
        return np.exp2(np.random.permutation(np.resize(levels, k // 32))).repeat(32)
    a = np.empty((k // 512, 16))
    for p in range(k // 512):
        a[p, :8] = np.random.permutation(np.resize(levels, 8))
        for g in range(8):
            far = levels[np.abs(levels - a[p, g]) >= 10]
            a[p, g + 8] = far[np.random.randint(len(far))]
    return np.exp2(a.ravel()).repeat(32)


def f64(x):
    return np.asarray(x).astype(np.float64)


def striped(idx):
    return np.tile(np.asarray(idx).reshape(-1, 16).T, (8, 1)).astype(np.uint16)


def unstriped(offs):
    return offs[:16].T.reshape(-1).astype(np.int64)


E2M1 = np.array([0.0, 0.5, 1.0, 1.5, 2.0, 3.0, 4.0, 6.0, -0.0, -0.5, -1.0, -1.5, -2.0, -3.0, -4.0, -6.0])


def pack_weight(w, fmt):
    k, n = w.shape
    w = f64(np.asarray(w, np.float32).astype(ml_dtypes.bfloat16)).reshape(k // 32, 32, n)
    amax = np.abs(w).max(1)
    if fmt in ("e4m3", "e5m2"):
        byte = np.frexp(amax)[1] - 1 + 127 - (7 if fmt == "e4m3" else 14)
    else:
        mant, ex = np.frexp(amax / 6.0)
        byte = np.where(mant > 0.5, ex, ex - 1) + 127
    byte = np.clip(np.where(amax > 0, byte, 1), 1, 254)
    scaled = (w * np.exp2(127.0 - byte)[:, None, :]).reshape(k, n).astype(np.float32)
    by_word = np.ascontiguousarray(scaled.reshape(k // 512, 128, 4, n).transpose(0, 1, 3, 2))
    if fmt in ("e4m3", "e5m2"):
        words = by_word.astype(ml_dtypes.float8_e4m3fn if fmt == "e4m3" else ml_dtypes.float8_e5m2).view(np.uint8)
    else:
        c = by_word.astype(ml_dtypes.float4_e2m1fn).view(np.uint8) & 0xF
        words = (c[..., 0::2] | (c[..., 1::2] << 4)).reshape(k // 512, 128, 2 * n)
    return np.ascontiguousarray(words), np.ascontiguousarray(byte.astype(np.uint8).reshape(k // 512, 16, n))


def unpack_weight(words, scales, fmt):
    g, _, n = scales.shape
    words = np.ascontiguousarray(words).reshape(g, 128, n, -1)
    if fmt in ("e4m3", "e5m2"):
        vals = words.view(ml_dtypes.float8_e4m3fn if fmt == "e4m3" else ml_dtypes.float8_e5m2).astype(np.float64)
    else:
        nib = np.empty((g, 128, n, 4), np.uint8)
        nib[..., 0::2] = words & 0xF
        nib[..., 1::2] = words >> 4
        vals = E2M1[nib]
    vals = vals * np.repeat(np.exp2(scales.astype(np.float64) - 127.0), 8, axis=1)[..., None]
    return vals.transpose(0, 1, 3, 2).reshape(g * 512, n)


K, T, J, R, F, Z, O, N, E = 512, 1024, 256, 512, 512, 1024, 128, 256, 1024


def setup_inputs():
    n = np.random.standard_normal
    idx = np.random.permutation(T)[:J]
    idx2 = np.random.permutation(Z)[:J]
    idx3 = np.random.permutation(J)[:O]
    idx4 = np.random.permutation(J)[:O]
    idx5 = np.random.permutation(E)[:O]
    fk = mx_kscale(K)
    fr = mx_kscale(R)
    ff = mx_kscale(F)
    wp = pack_weight(n((K, R)) * 1 / np.sqrt(K) / fk[:, None] * fr, "e2m1")
    xop = pack_weight(n((F, Z)) / ff[:, None], "e2m1")
    w2p = pack_weight(n((F, R)) * 1 / np.sqrt(F) * ff[:, None] * fr, "e5m2")
    wbp = pack_weight(n((R, N)) * 1 / np.sqrt(R) / fr[:, None], "e5m2")
    return {
        "cq": (np.random.randint(-7, 8, (K, T)).astype(np.float64)).astype(np.float32),
        "ga": (np.random.uniform(0.1, 0.4, (K, 1)) * fk[:, None]).astype(np.float32),
        "w_words": wp[0],
        "w_scales": wp[1],
        "xo_words": xop[0],
        "xo_scales": xop[1],
        "w2_words": w2p[0],
        "w2_scales": w2p[1],
        "sa": (np.random.uniform(0.5, 1.6, (R, 1))).astype(np.float32),
        "sb": (np.random.uniform(0.5, 1.6, (R, 1))).astype(np.float32),
        "wb_words": wbp[0],
        "wb_scales": wbp[1],
        "tz": (np.random.randint(-9, 10, (N, E)).astype(np.float64)).astype(np.float32),
        "so": (np.random.uniform(0.1, 0.3, (N, 1))).astype(np.float32),
        "offs": striped(idx),
        "offs2": striped(idx2),
        "offs3": striped(idx3),
        "offs4": striped(idx4),
        "offs5": striped(idx5),
    }


def reference(cq, ga, w_words, w_scales, xo_words, xo_scales, w2_words, w2_scales, sa, sb, wb_words, wb_scales, tz, so, offs, offs2, offs3, offs4, offs5):
    idx = unstriped(offs)
    idx2 = unstriped(offs2)
    idx3 = unstriped(offs3)
    idx4 = unstriped(offs4)
    idx5 = unstriped(offs5)
    wu = unpack_weight(w_words, w_scales, "e2m1")
    xou = unpack_weight(xo_words, xo_scales, "e2m1")
    w2u = unpack_weight(w2_words, w2_scales, "e5m2")
    wbu = unpack_weight(wb_words, wb_scales, "e5m2")
    x1 = f64(cq)[:, idx] * f64(ga)
    x1q = mxq(x1, 0, "e4m3")
    a = wu.T @ x1q
    xoidx2g = xou[:, idx2]
    b = w2u.T @ xoidx2g
    hid = np.maximum(a[:, idx3] * f64(sa), b[:, idx4] * f64(sb))
    hidq = mxq(hid, 0, "e4m3")
    p = wbu.T @ hidq
    y = np.maximum(p, f64(tz)[:, idx5] * f64(so))
    return y

@@ -1,0 +1,200 @@
+from contextlib import ExitStack
+
+import concourse.mybir as mybir
+
+K, T, J, R, F, Z, O, N, E = 512, 1024, 256, 512, 512, 1024, 128, 256, 1024
+FLOPS = 2 * (K * R * J + F * R * J + R * N * O)
+
+F32 = mybir.dt.float32
+BF16 = mybir.dt.bfloat16
+I32 = mybir.dt.int32
+U32 = mybir.dt.uint32
+U16 = mybir.dt.uint16
+U8 = mybir.dt.uint8
+E4M3 = mybir.dt.float8_e4m3fn_x4
+E5M2 = mybir.dt.float8_e5m2_x4
+E2M1 = mybir.dt.float4_e2m1fn_x4
+COPY = mybir.ActivationFunctionType.Copy
+MAX = mybir.AluOpType.max
+
+P = 128
+PACK = 4
+QUAD = 32
+HALF = 64
+
+
+def tile_list_weighedboth_codednote_one_stepfloor_kernel(
+    tc, cq, ga, w_words, w_scales, xo_words, xo_scales, w2_words, w2_scales, sa, sb,
+    wb_words, wb_scales, tz, so, offs, offs2, offs3, offs4, offs5, out,
+):
+    nc = tc.nc
+    with ExitStack() as ctx:
+        sb_pool = ctx.enter_context(tc.tile_pool(name="held", bufs=1))
+        ps_pool = ctx.enter_context(tc.psum_pool(name="banks", bufs=1))
+
+        def tile(name, shape, dtype):
+            return sb_pool.tile(shape, dtype, name=name, align_bytes=64)
+
+        list1 = tile("list1", [P, J // 16], U16)
+        list2 = tile("list2", [P, J // 16], U16)
+        list3 = tile("list3", [P, O // 16], U16)
+        list4 = tile("list4", [P, O // 16], U16)
+        list5 = tile("list5", [P, O // 16], U16)
+        ga_t = tile("ga_t", [P, PACK], F32)
+        sa_t = tile("sa_t", [P, PACK], F32)
+        sb_t = tile("sb_t", [P, PACK], F32)
+        so_t = tile("so_t", [P, N // P], F32)
+        cq_t = [tile("cq%d" % t, [P, T], F32) for t in range(PACK)]
+        tz_t = [tile("tz%d" % h, [P, E], F32) for h in range(N // P)]
+        xo_w = tile("xo_w", [P, Z], U16)
+        xo_s = tile("xo_s", [P, Z], U8)
+        xo_stage = tile("xo_stage", [P, 2, Z // 4], I32)
+        w_raw = tile("w_raw", [P, R], U16)
+        w_sraw = tile("w_sraw", [P, R], U8)
+        w2_raw = tile("w2_raw", [P, R], U32)
+        w2_stage = tile("w2_stage", [P, 2, R // 4], I32)
+        w2_sraw = tile("w2_sraw", [P, R], U8)
+        wb_w = tile("wb_w", [P, N], U32)
+        wb_s = tile("wb_s", [P, N], U8)
+
+        nc.vector.memset(xo_stage[0:HALF, :, :], 0)
+        nc.vector.memset(w2_stage[HALF:P, :, :], 0)
+        nc.vector.memset(w_sraw[:].bitcast(I32), 0)
+        nc.vector.memset(wb_s[:].bitcast(I32), 0)
+
+        def stage_scale_rows(stage, first, scales):
+            rows = scales[0].bitcast(I32).rearrange("(g q r) c -> q r g c", g=2, r=PACK)
+            for q in range(2):
+                nc.scalar.dma_start(out=stage[first + QUAD * q : first + QUAD * q + PACK, :, :], in_=rows[q])
+
+        def spread_scale_rows(plane, stage, first):
+            for g in range(2):
+                nc.vector.tensor_copy(
+                    out=plane[HALF * g : HALF * (g + 1), :].bitcast(I32), in_=stage[first : first + HALF, g, :]
+                )
+
+        def dealt(vec):
+            return vec.rearrange("(p t) o -> p (t o)", t=PACK)
+
+        def load_scale_rows(plane, scales):
+            for q in range(PACK):
+                nc.sync.dma_start(
+                    out=plane[QUAD * q : QUAD * q + PACK, :].bitcast(I32),
+                    in_=scales[0, PACK * q : PACK * (q + 1), :].bitcast(I32),
+                )
+
+        stage_scale_rows(xo_stage, 0, xo_scales)
+        stage_scale_rows(w2_stage, HALF, w2_scales)
+        nc.gpsimd.dma_start(out=ga_t[:], in_=dealt(ga))
+        nc.gpsimd.dma_start(out=sb_t[:], in_=dealt(sb))
+        nc.gpsimd.dma_start(out=sa_t[:], in_=dealt(sa))
+        with nc.allow_non_contiguous_dma(reason="one value a partition"):
+            nc.gpsimd.dma_start(out=so_t[:], in_=so.rearrange("(h p) o -> p (h o)", p=P))
+
+        cq_rows = cq.rearrange("(p t) e -> t p e", t=PACK)
+        nc.sync.dma_start(out=xo_w[:].bitcast(I32), in_=xo_words[0].bitcast(I32))
+        nc.sync.dma_start(out=list2[:], in_=offs2)
+        nc.sync.dma_start(out=w2_raw[:].bitcast(I32), in_=w2_words[0].rearrange("p c b -> p (c b)").bitcast(I32))
+        nc.sync.dma_start(out=cq_t[0][:], in_=cq_rows[0])
+        nc.sync.dma_start(out=list1[:], in_=offs)
+        nc.sync.dma_start(out=cq_t[1][:], in_=cq_rows[1])
+        load_scale_rows(w_sraw, w_scales)
+        nc.sync.dma_start(out=cq_t[2][:], in_=cq_rows[2])
+        nc.sync.dma_start(out=cq_t[3][:], in_=cq_rows[3])
+        nc.sync.dma_start(out=w_raw[:].bitcast(I32), in_=w_words[0].bitcast(I32))
+        nc.sync.dma_start(out=list4[:], in_=offs4)
+        nc.sync.dma_start(out=list3[:], in_=offs3)
+        for h in range(N // P):
+            nc.sync.dma_start(out=tz_t[h][:], in_=tz[h * P : (h + 1) * P, :])
+        nc.sync.dma_start(out=list5[:], in_=offs5)
+        nc.sync.dma_start(out=wb_w[:].bitcast(I32), in_=wb_words[0].rearrange("p c b -> p (c b)").bitcast(I32))
+        load_scale_rows(wb_s, wb_scales)
+
+        def deal_columns(copy, dst, src):
+            copy(out=dst[:].rearrange("p t m -> p m t"), in_=src[:].rearrange("p (m t) -> p m t", t=PACK))
+
+        x1_planes = [tile("x1_planes%d" % u, [P, 2, J], BF16) for u in range(2)]
+        x1_grouped = tile("x1_grouped", [P, J, PACK], BF16)
+        x1_codes = tile("x1_codes", [P, J], U32)
+        x1_scales = tile("x1_scales", [P, J], U8)
+        for u in range(2):
+            for v in range(2):
+                t = 2 * u + v
+                nc.scalar.activation(
+                    out=x1_planes[u][:, v, :], in_=cq_t[t][:].indirect(list1[:]), func=COPY, scale=ga_t[:, t : t + 1]
+                )
+            nc.vector.tensor_copy(out=x1_grouped[:, :, 2 * u : 2 * u + 2], in_=x1_planes[u][:].rearrange("p v j -> p j v"))
+        nc.vector.quantize_mx(
+            out=x1_codes[:].bitcast(E4M3), scales=x1_scales[:], in_=x1_grouped[:].rearrange("p j t -> p (j t)")
+        )
+
+        w_dealt = tile("w_dealt", [P, PACK, P], U16)
+        w_sdealt = tile("w_sdealt", [P, PACK, P], U8)
+        deal_columns(nc.scalar.copy, w_dealt, w_raw)
+        deal_columns(nc.vector.tensor_copy, w_sdealt, w_sraw)
+        a_bank = [ps_pool.tile([P, J], F32, name="a_bank%d" % t) for t in range(PACK)]
+        a_t = [tile("a%d" % t, [P, J], F32) for t in range(PACK)]
+        for t in range(PACK):
+            nc.tensor.matmul_mx(
+                out=a_bank[t][:], lhsT=w_dealt[:, t, :].bitcast(E2M1), lhsT_scale=w_sdealt[:, t, :],
+                rhs=x1_codes[:].bitcast(E4M3), rhs_scale=x1_scales[:], start=True, stop=True,
+            )
+            nc.vector.tensor_copy(out=a_t[t][:], in_=a_bank[t][:])
+
+        xo_gw = tile("xo_gw", [P, J], U16)
+        xo_gs = tile("xo_gs", [P, J], U8)
+        nc.vector.tensor_copy(out=xo_gw[:], in_=xo_w[:].indirect(list2[:]))
+        spread_scale_rows(xo_s, xo_stage, 0)
+        nc.vector.tensor_copy(out=xo_gs[:], in_=xo_s[:].indirect(list2[:]))
+        spread_scale_rows(w2_sraw, w2_stage, HALF)
+        w2_dealt = tile("w2_dealt", [P, PACK, P], U32)
+        w2_sdealt = tile("w2_sdealt", [P, PACK, P], U8)
+        deal_columns(nc.scalar.copy, w2_dealt, w2_raw)
+        deal_columns(nc.vector.tensor_copy, w2_sdealt, w2_sraw)
+        b_bank = [ps_pool.tile([P, 2, J], F32, name="b_bank%d" % u) for u in range(2)]
+        b_t = [tile("b%d" % t, [P, J], F32) for t in range(PACK)]
+        b_picked = [tile("b_picked%d" % u, [P, 2, O], F32) for u in range(2)]
+        for u in range(2):
+            for v in range(2):
+                t = 2 * u + v
+                nc.tensor.matmul_mx(
+                    out=b_bank[u][:, v, :], lhsT=w2_dealt[:, t, :].bitcast(E5M2), lhsT_scale=w2_sdealt[:, t, :],
+                    rhs=xo_gw[:].bitcast(E2M1), rhs_scale=xo_gs[:], start=True, stop=True,
+                )
+            for v in range(2):
+                nc.vector.tensor_copy(out=b_t[2 * u + v][:], in_=b_bank[u][:, v, :])
+        for t in range(PACK):
+            nc.scalar.activation(
+                out=b_picked[t // 2][:, t % 2, :], in_=b_t[t][:].indirect(list4[:]), func=COPY, scale=sb_t[:, t : t + 1]
+            )
+
+        a_picked = [tile("a_picked%d" % u, [P, 2, O], F32) for u in range(2)]
+        hid_grouped = tile("hid_grouped", [P, O, PACK], BF16)
+        hid_codes = tile("hid_codes", [P, O], U32)
+        hid_scales = tile("hid_scales", [P, O], U8)
+        for u in range(2):
+            for v in range(2):
+                t = 2 * u + v
+                nc.scalar.activation(
+                    out=a_picked[u][:, v, :], in_=a_t[t][:].indirect(list3[:]), func=COPY, scale=sa_t[:, t : t + 1]
+                )
+            nc.vector.tensor_tensor(
+                out=hid_grouped[:, :, 2 * u : 2 * u + 2], in0=a_picked[u][:].rearrange("p v o -> p o v"),
+                in1=b_picked[u][:].rearrange("p v o -> p o v"), op=MAX,
+            )
+        nc.vector.quantize_mx(
+            out=hid_codes[:].bitcast(E4M3), scales=hid_scales[:], in_=hid_grouped[:].rearrange("p o t -> p (o t)")
+        )
+
+        for h in range(N // P):
+            cols = slice(h * P, (h + 1) * P)
+            floor_t = tile("floor%d" % h, [P, O], F32)
+            y_t = tile("y%d" % h, [P, O], F32)
+            p_bank = ps_pool.tile([P, O], F32, name="p_bank%d" % h)
+            nc.scalar.activation(out=floor_t[:], in_=tz_t[h][:].indirect(list5[:]), func=COPY, scale=so_t[:, h : h + 1])
+            nc.tensor.matmul_mx(
+                out=p_bank[:], lhsT=wb_w[:, cols].bitcast(E5M2), lhsT_scale=wb_s[:, cols],
+                rhs=hid_codes[:].bitcast(E4M3), rhs_scale=hid_scales[:], start=True, stop=True,
+            )
+            nc.vector.tensor_tensor(out=y_t[:], in0=p_bank[:], in1=floor_t[:], op=MAX)
+            nc.sync.dma_start(out=out[cols, :], in_=y_t[:])

@@ -19,8 +19,12 @@ MAX = mybir.AluOpType.max
 
 P = 128
 PACK = 4
-QUAD = 32
-HALF = 64
+QUADRANT = 32
+QUADRANTS = P // QUADRANT
+HALF = P // 2
+LIST_GROUP = 16
+LINE_BYTES = 16
+WORD_BYTES = 4
 
 
 def tile_list_weighedboth_codednote_one_stepfloor_kernel(
@@ -29,17 +33,17 @@ def tile_list_weighedboth_codednote_one_stepfloor_kernel(
 ):
     nc = tc.nc
     with ExitStack() as ctx:
-        sb_pool = ctx.enter_context(tc.tile_pool(name="held", bufs=1))
-        ps_pool = ctx.enter_context(tc.psum_pool(name="banks", bufs=1))
+        held = ctx.enter_context(tc.tile_pool(name="held", bufs=1))
+        banks = ctx.enter_context(tc.psum_pool(name="banks", bufs=1))
 
         def tile(name, shape, dtype):
-            return sb_pool.tile(shape, dtype, name=name, align_bytes=64)
+            return held.tile(shape, dtype, name=name, align_bytes=64)
 
-        list1 = tile("list1", [P, J // 16], U16)
-        list2 = tile("list2", [P, J // 16], U16)
-        list3 = tile("list3", [P, O // 16], U16)
-        list4 = tile("list4", [P, O // 16], U16)
-        list5 = tile("list5", [P, O // 16], U16)
+        list1 = tile("list1", [P, J // LIST_GROUP], U16)
+        list2 = tile("list2", [P, J // LIST_GROUP], U16)
+        list3 = tile("list3", [P, O // LIST_GROUP], U16)
+        list4 = tile("list4", [P, O // LIST_GROUP], U16)
+        list5 = tile("list5", [P, O // LIST_GROUP], U16)
         ga_t = tile("ga_t", [P, PACK], F32)
         sa_t = tile("sa_t", [P, PACK], F32)
         sb_t = tile("sb_t", [P, PACK], F32)
@@ -48,60 +52,60 @@ def tile_list_weighedboth_codednote_one_stepfloor_kernel(
         tz_t = [tile("tz%d" % h, [P, E], F32) for h in range(N // P)]
         xo_w = tile("xo_w", [P, Z], U16)
         xo_s = tile("xo_s", [P, Z], U8)
-        xo_stage = tile("xo_stage", [P, 2, Z // 4], I32)
-        w_raw = tile("w_raw", [P, R], U16)
-        w_sraw = tile("w_sraw", [P, R], U8)
-        w2_raw = tile("w2_raw", [P, R], U32)
-        w2_stage = tile("w2_stage", [P, 2, R // 4], I32)
-        w2_sraw = tile("w2_sraw", [P, R], U8)
+        xo_stage = tile("xo_stage", [P, 2, Z // WORD_BYTES], I32)
+        w_w = tile("w_w", [P, R], U16)
+        w_s = tile("w_s", [P, R], U8)
+        w2_w = tile("w2_w", [P, R], U32)
+        w2_stage = tile("w2_stage", [P, 2, R // WORD_BYTES], I32)
+        w2_s = tile("w2_s", [P, R], U8)
         wb_w = tile("wb_w", [P, N], U32)
         wb_s = tile("wb_s", [P, N], U8)
 
         nc.vector.memset(xo_stage[0:HALF, :, :], 0)
         nc.vector.memset(w2_stage[HALF:P, :, :], 0)
-        nc.vector.memset(w_sraw[:].bitcast(I32), 0)
+        nc.vector.memset(w_s[:].bitcast(I32), 0)
         nc.vector.memset(wb_s[:].bitcast(I32), 0)
+
+        def by_slice(vec):
+            return vec.rearrange("(p t) o -> p (t o)", t=PACK)
 
         def stage_scale_rows(stage, first, scales):
             rows = scales[0].bitcast(I32).rearrange("(g q r) c -> q r g c", g=2, r=PACK)
             for q in range(2):
-                nc.scalar.dma_start(out=stage[first + QUAD * q : first + QUAD * q + PACK, :, :], in_=rows[q])
+                nc.sync.dma_start(out=stage[first + QUADRANT * q : first + QUADRANT * q + PACK, :, :], in_=rows[q])
 
-        def spread_scale_rows(plane, stage, first):
+        def spread_scale_rows(scale_tile, stage, first):
             for g in range(2):
                 nc.vector.tensor_copy(
-                    out=plane[HALF * g : HALF * (g + 1), :].bitcast(I32), in_=stage[first : first + HALF, g, :]
+                    out=scale_tile[HALF * g : HALF * (g + 1), :].bitcast(I32), in_=stage[first : first + HALF, g, :]
                 )
 
-        def dealt(vec):
-            return vec.rearrange("(p t) o -> p (t o)", t=PACK)
-
-        def load_scale_rows(plane, scales):
-            for q in range(PACK):
+        def load_scale_rows(scale_tile, scales):
+            for q in range(QUADRANTS):
                 nc.sync.dma_start(
-                    out=plane[QUAD * q : QUAD * q + PACK, :].bitcast(I32),
+                    out=scale_tile[QUADRANT * q : QUADRANT * q + PACK, :].bitcast(I32),
                     in_=scales[0, PACK * q : PACK * (q + 1), :].bitcast(I32),
                 )
 
-        stage_scale_rows(xo_stage, 0, xo_scales)
-        stage_scale_rows(w2_stage, HALF, w2_scales)
-        nc.gpsimd.dma_start(out=ga_t[:], in_=dealt(ga))
-        nc.gpsimd.dma_start(out=sb_t[:], in_=dealt(sb))
-        nc.gpsimd.dma_start(out=sa_t[:], in_=dealt(sa))
-        with nc.allow_non_contiguous_dma(reason="one value a partition"):
+        nc.gpsimd.dma_start(out=ga_t[:], in_=by_slice(ga))
+        nc.gpsimd.dma_start(out=sb_t[:], in_=by_slice(sb))
+        nc.gpsimd.dma_start(out=sa_t[:], in_=by_slice(sa))
+        with nc.allow_non_contiguous_dma(reason="two values a partition, 128 rows apart"):
             nc.gpsimd.dma_start(out=so_t[:], in_=so.rearrange("(h p) o -> p (h o)", p=P))
 
         cq_rows = cq.rearrange("(p t) e -> t p e", t=PACK)
         nc.sync.dma_start(out=xo_w[:].bitcast(I32), in_=xo_words[0].bitcast(I32))
         nc.sync.dma_start(out=list2[:], in_=offs2)
-        nc.sync.dma_start(out=w2_raw[:].bitcast(I32), in_=w2_words[0].rearrange("p c b -> p (c b)").bitcast(I32))
+        nc.sync.dma_start(out=w2_w[:].bitcast(I32), in_=w2_words[0].rearrange("p c b -> p (c b)").bitcast(I32))
+        stage_scale_rows(xo_stage, 0, xo_scales)
+        stage_scale_rows(w2_stage, HALF, w2_scales)
         nc.sync.dma_start(out=cq_t[0][:], in_=cq_rows[0])
         nc.sync.dma_start(out=list1[:], in_=offs)
         nc.sync.dma_start(out=cq_t[1][:], in_=cq_rows[1])
-        load_scale_rows(w_sraw, w_scales)
+        load_scale_rows(w_s, w_scales)
         nc.sync.dma_start(out=cq_t[2][:], in_=cq_rows[2])
         nc.sync.dma_start(out=cq_t[3][:], in_=cq_rows[3])
-        nc.sync.dma_start(out=w_raw[:].bitcast(I32), in_=w_words[0].bitcast(I32))
+        nc.sync.dma_start(out=w_w[:].bitcast(I32), in_=w_words[0].bitcast(I32))
         nc.sync.dma_start(out=list4[:], in_=offs4)
         nc.sync.dma_start(out=list3[:], in_=offs3)
         for h in range(N // P):
@@ -110,56 +114,69 @@ def tile_list_weighedboth_codednote_one_stepfloor_kernel(
         nc.sync.dma_start(out=wb_w[:].bitcast(I32), in_=wb_words[0].rearrange("p c b -> p (c b)").bitcast(I32))
         load_scale_rows(wb_s, wb_scales)
 
-        def deal_columns(copy, dst, src):
-            copy(out=dst[:].rearrange("p t m -> p m t"), in_=src[:].rearrange("p (m t) -> p m t", t=PACK))
+        def deal_columns(copy, dealt, src, element_bytes):
+            run = LINE_BYTES // element_bytes
+            copy(
+                out=dealt[:].rearrange("p t (c i) -> p c t i", i=run),
+                in_=src[:].rearrange("p (c i t) -> p c t i", i=run, t=PACK),
+            )
 
-        x1_planes = [tile("x1_planes%d" % u, [P, 2, J], BF16) for u in range(2)]
-        x1_grouped = tile("x1_grouped", [P, J, PACK], BF16)
+        x1_pair = [tile("x1_pair%d" % u, [P, 2, J], BF16) for u in range(2)]
+        x1_woven = [tile("x1_woven%d" % s, [P, P, PACK], BF16) for s in range(2)]
         x1_codes = tile("x1_codes", [P, J], U32)
         x1_scales = tile("x1_scales", [P, J], U8)
         for u in range(2):
             for v in range(2):
                 t = 2 * u + v
                 nc.scalar.activation(
-                    out=x1_planes[u][:, v, :], in_=cq_t[t][:].indirect(list1[:]), func=COPY, scale=ga_t[:, t : t + 1]
+                    out=x1_pair[u][:, v, :], in_=cq_t[t][:].indirect(list1[:]), func=COPY, scale=ga_t[:, t : t + 1]
                 )
-            nc.vector.tensor_copy(out=x1_grouped[:, :, 2 * u : 2 * u + 2], in_=x1_planes[u][:].rearrange("p v j -> p j v"))
-        nc.vector.quantize_mx(
-            out=x1_codes[:].bitcast(E4M3), scales=x1_scales[:], in_=x1_grouped[:].rearrange("p j t -> p (j t)")
-        )
+            for s in range(2):
+                nc.vector.tensor_copy(
+                    out=x1_woven[s][:, :, 2 * u : 2 * u + 2],
+                    in_=x1_pair[u][:, :, s * P : (s + 1) * P].rearrange("p v j -> p j v"),
+                )
+        for s in range(2):
+            nc.vector.quantize_mx(
+                out=x1_codes[:, s * P : (s + 1) * P].bitcast(E4M3), scales=x1_scales[:, s * P : (s + 1) * P],
+                in_=x1_woven[s][:].rearrange("p j t -> p (j t)"),
+            )
 
         w_dealt = tile("w_dealt", [P, PACK, P], U16)
-        w_sdealt = tile("w_sdealt", [P, PACK, P], U8)
-        deal_columns(nc.scalar.copy, w_dealt, w_raw)
-        deal_columns(nc.vector.tensor_copy, w_sdealt, w_sraw)
-        a_bank = [ps_pool.tile([P, J], F32, name="a_bank%d" % t) for t in range(PACK)]
+        w_s_dealt = tile("w_s_dealt", [P, PACK, P], U8)
+        deal_columns(nc.scalar.copy, w_dealt, w_w, 2)
+        deal_columns(nc.vector.tensor_copy, w_s_dealt, w_s, 1)
         a_t = [tile("a%d" % t, [P, J], F32) for t in range(PACK)]
         for t in range(PACK):
-            nc.tensor.matmul_mx(
-                out=a_bank[t][:], lhsT=w_dealt[:, t, :].bitcast(E2M1), lhsT_scale=w_sdealt[:, t, :],
-                rhs=x1_codes[:].bitcast(E4M3), rhs_scale=x1_scales[:], start=True, stop=True,
-            )
-            nc.vector.tensor_copy(out=a_t[t][:], in_=a_bank[t][:])
+            width = P if t == 0 else J
+            for start in range(0, J, width):
+                slots = slice(start, start + width)
+                a_bank = banks.tile([P, width], F32, name="a_bank%d_%d" % (t, start))
+                nc.tensor.matmul_mx(
+                    out=a_bank[:], lhsT=w_dealt[:, t, :].bitcast(E2M1), lhsT_scale=w_s_dealt[:, t, :],
+                    rhs=x1_codes[:, slots].bitcast(E4M3), rhs_scale=x1_scales[:, slots], start=True, stop=True,
+                )
+                nc.vector.tensor_copy(out=a_t[t][:, slots], in_=a_bank[:])
 
-        xo_gw = tile("xo_gw", [P, J], U16)
-        xo_gs = tile("xo_gs", [P, J], U8)
-        nc.vector.tensor_copy(out=xo_gw[:], in_=xo_w[:].indirect(list2[:]))
+        xo_w_picked = tile("xo_w_picked", [P, J], U16)
+        xo_s_picked = tile("xo_s_picked", [P, J], U8)
+        nc.vector.tensor_copy(out=xo_w_picked[:], in_=xo_w[:].indirect(list2[:]))
         spread_scale_rows(xo_s, xo_stage, 0)
-        nc.vector.tensor_copy(out=xo_gs[:], in_=xo_s[:].indirect(list2[:]))
-        spread_scale_rows(w2_sraw, w2_stage, HALF)
+        nc.vector.tensor_copy(out=xo_s_picked[:], in_=xo_s[:].indirect(list2[:]))
+        spread_scale_rows(w2_s, w2_stage, HALF)
         w2_dealt = tile("w2_dealt", [P, PACK, P], U32)
-        w2_sdealt = tile("w2_sdealt", [P, PACK, P], U8)
-        deal_columns(nc.scalar.copy, w2_dealt, w2_raw)
-        deal_columns(nc.vector.tensor_copy, w2_sdealt, w2_sraw)
-        b_bank = [ps_pool.tile([P, 2, J], F32, name="b_bank%d" % u) for u in range(2)]
+        w2_s_dealt = tile("w2_s_dealt", [P, PACK, P], U8)
+        deal_columns(nc.scalar.copy, w2_dealt, w2_w, 4)
+        deal_columns(nc.vector.tensor_copy, w2_s_dealt, w2_s, 1)
+        b_bank = [banks.tile([P, 2, J], F32, name="b_bank%d" % u, tag="b_then_p%d" % u) for u in range(2)]
         b_t = [tile("b%d" % t, [P, J], F32) for t in range(PACK)]
         b_picked = [tile("b_picked%d" % u, [P, 2, O], F32) for u in range(2)]
         for u in range(2):
             for v in range(2):
                 t = 2 * u + v
                 nc.tensor.matmul_mx(
-                    out=b_bank[u][:, v, :], lhsT=w2_dealt[:, t, :].bitcast(E5M2), lhsT_scale=w2_sdealt[:, t, :],
-                    rhs=xo_gw[:].bitcast(E2M1), rhs_scale=xo_gs[:], start=True, stop=True,
+                    out=b_bank[u][:, v, :], lhsT=w2_dealt[:, t, :].bitcast(E5M2), lhsT_scale=w2_s_dealt[:, t, :],
+                    rhs=xo_w_picked[:].bitcast(E2M1), rhs_scale=xo_s_picked[:], start=True, stop=True,
                 )
             for v in range(2):
                 nc.vector.tensor_copy(out=b_t[2 * u + v][:], in_=b_bank[u][:, v, :])
@@ -169,7 +186,7 @@ def tile_list_weighedboth_codednote_one_stepfloor_kernel(
             )
 
         a_picked = [tile("a_picked%d" % u, [P, 2, O], F32) for u in range(2)]
-        hid_grouped = tile("hid_grouped", [P, O, PACK], BF16)
+        hid_woven = tile("hid_woven", [P, O, PACK], BF16)
         hid_codes = tile("hid_codes", [P, O], U32)
         hid_scales = tile("hid_scales", [P, O], U8)
         for u in range(2):
@@ -179,22 +196,22 @@ def tile_list_weighedboth_codednote_one_stepfloor_kernel(
                     out=a_picked[u][:, v, :], in_=a_t[t][:].indirect(list3[:]), func=COPY, scale=sa_t[:, t : t + 1]
                 )
             nc.vector.tensor_tensor(
-                out=hid_grouped[:, :, 2 * u : 2 * u + 2], in0=a_picked[u][:].rearrange("p v o -> p o v"),
+                out=hid_woven[:, :, 2 * u : 2 * u + 2], in0=a_picked[u][:].rearrange("p v o -> p o v"),
                 in1=b_picked[u][:].rearrange("p v o -> p o v"), op=MAX,
             )
         nc.vector.quantize_mx(
-            out=hid_codes[:].bitcast(E4M3), scales=hid_scales[:], in_=hid_grouped[:].rearrange("p o t -> p (o t)")
+            out=hid_codes[:].bitcast(E4M3), scales=hid_scales[:], in_=hid_woven[:].rearrange("p o t -> p (o t)")
         )
 
         for h in range(N // P):
-            cols = slice(h * P, (h + 1) * P)
+            features = slice(h * P, (h + 1) * P)
             floor_t = tile("floor%d" % h, [P, O], F32)
             y_t = tile("y%d" % h, [P, O], F32)
-            p_bank = ps_pool.tile([P, O], F32, name="p_bank%d" % h)
+            p_bank = banks.tile([P, O], F32, name="p_bank%d" % h, tag="b_then_p%d" % h)
             nc.scalar.activation(out=floor_t[:], in_=tz_t[h][:].indirect(list5[:]), func=COPY, scale=so_t[:, h : h + 1])
             nc.tensor.matmul_mx(
-                out=p_bank[:], lhsT=wb_w[:, cols].bitcast(E5M2), lhsT_scale=wb_s[:, cols],
+                out=p_bank[:], lhsT=wb_w[:, features].bitcast(E5M2), lhsT_scale=wb_s[:, features],
                 rhs=hid_codes[:].bitcast(E4M3), rhs_scale=hid_scales[:], start=True, stop=True,
             )
             nc.vector.tensor_tensor(out=y_t[:], in0=p_bank[:], in1=floor_t[:], op=MAX)
-            nc.sync.dma_start(out=out[cols, :], in_=y_t[:])
+            nc.sync.dma_start(out=out[features, :], in_=y_t[:])

from contextlib import ExitStack

import concourse.mybir as mybir

K, T, J, R, F, Z, O, N, E = 512, 1024, 256, 512, 512, 1024, 128, 256, 1024
FLOPS = 2 * (K * R * J + F * R * J + R * N * O)

F32 = mybir.dt.float32
BF16 = mybir.dt.bfloat16
I32 = mybir.dt.int32
U32 = mybir.dt.uint32
U16 = mybir.dt.uint16
U8 = mybir.dt.uint8
E4M3 = mybir.dt.float8_e4m3fn_x4
E5M2 = mybir.dt.float8_e5m2_x4
E2M1 = mybir.dt.float4_e2m1fn_x4
COPY = mybir.ActivationFunctionType.Copy
MAX = mybir.AluOpType.max

P = 128
PACK = 4
QUADRANT = 32
QUADRANTS = P // QUADRANT
HALF = P // 2
LIST_GROUP = 16
LINE_BYTES = 16
WORD_BYTES = 4


def tile_list_weighedboth_codednote_one_stepfloor_kernel(
    tc, cq, ga, w_words, w_scales, xo_words, xo_scales, w2_words, w2_scales, sa, sb,
    wb_words, wb_scales, tz, so, offs, offs2, offs3, offs4, offs5, out,
):
    nc = tc.nc
    with ExitStack() as ctx:
        held = ctx.enter_context(tc.tile_pool(name="held", bufs=1))
        banks = ctx.enter_context(tc.psum_pool(name="banks", bufs=1))

        def tile(name, shape, dtype):
            return held.tile(shape, dtype, name=name, align_bytes=64)

        list1 = tile("list1", [P, J // LIST_GROUP], U16)
        list2 = tile("list2", [P, J // LIST_GROUP], U16)
        list3 = tile("list3", [P, O // LIST_GROUP], U16)
        list4 = tile("list4", [P, O // LIST_GROUP], U16)
        list5 = tile("list5", [P, O // LIST_GROUP], U16)
        ga_t = tile("ga_t", [P, PACK], F32)
        sa_t = tile("sa_t", [P, PACK], F32)
        sb_t = tile("sb_t", [P, PACK], F32)
        so_t = tile("so_t", [P, N // P], F32)
        cq_t = [tile("cq%d" % t, [P, T], F32) for t in range(PACK)]
        tz_t = [tile("tz%d" % h, [P, E], F32) for h in range(N // P)]
        xo_w = tile("xo_w", [P, Z], U16)
        xo_s = tile("xo_s", [P, Z], U8)
        xo_stage = tile("xo_stage", [P, 2, Z // WORD_BYTES], I32)
        w_w = tile("w_w", [P, R], U16)
        w_s = tile("w_s", [P, R], U8)
        w2_w = tile("w2_w", [P, R], U32)
        w2_stage = tile("w2_stage", [P, 2, R // WORD_BYTES], I32)
        w2_s = tile("w2_s", [P, R], U8)
        wb_w = tile("wb_w", [P, N], U32)
        wb_s = tile("wb_s", [P, N], U8)

        nc.vector.memset(xo_stage[0:HALF, :, :], 0)
        nc.vector.memset(w2_stage[HALF:P, :, :], 0)
        nc.vector.memset(w_s[:].bitcast(I32), 0)
        nc.vector.memset(wb_s[:].bitcast(I32), 0)

        def by_slice(vec):
            return vec.rearrange("(p t) o -> p (t o)", t=PACK)

        def stage_scale_rows(stage, first, scales):
            rows = scales[0].bitcast(I32).rearrange("(g q r) c -> q r g c", g=2, r=PACK)
            for q in range(2):
                nc.sync.dma_start(out=stage[first + QUADRANT * q : first + QUADRANT * q + PACK, :, :], in_=rows[q])

        def spread_scale_rows(scale_tile, stage, first):
            for g in range(2):
                nc.vector.tensor_copy(
                    out=scale_tile[HALF * g : HALF * (g + 1), :].bitcast(I32), in_=stage[first : first + HALF, g, :]
                )

        def load_scale_rows(scale_tile, scales):
            for q in range(QUADRANTS):
                nc.sync.dma_start(
                    out=scale_tile[QUADRANT * q : QUADRANT * q + PACK, :].bitcast(I32),
                    in_=scales[0, PACK * q : PACK * (q + 1), :].bitcast(I32),
                )

        nc.gpsimd.dma_start(out=ga_t[:], in_=by_slice(ga))
        nc.gpsimd.dma_start(out=sb_t[:], in_=by_slice(sb))
        nc.gpsimd.dma_start(out=sa_t[:], in_=by_slice(sa))
        with nc.allow_non_contiguous_dma(reason="two values a partition, 128 rows apart"):
            nc.gpsimd.dma_start(out=so_t[:], in_=so.rearrange("(h p) o -> p (h o)", p=P))

        cq_rows = cq.rearrange("(p t) e -> t p e", t=PACK)
        nc.sync.dma_start(out=xo_w[:].bitcast(I32), in_=xo_words[0].bitcast(I32))
        nc.sync.dma_start(out=list2[:], in_=offs2)
        nc.sync.dma_start(out=w2_w[:].bitcast(I32), in_=w2_words[0].rearrange("p c b -> p (c b)").bitcast(I32))
        stage_scale_rows(xo_stage, 0, xo_scales)
        stage_scale_rows(w2_stage, HALF, w2_scales)
        nc.sync.dma_start(out=cq_t[0][:], in_=cq_rows[0])
        nc.sync.dma_start(out=list1[:], in_=offs)
        nc.sync.dma_start(out=cq_t[1][:], in_=cq_rows[1])
        load_scale_rows(w_s, w_scales)
        nc.sync.dma_start(out=cq_t[2][:], in_=cq_rows[2])
        nc.sync.dma_start(out=cq_t[3][:], in_=cq_rows[3])
        nc.sync.dma_start(out=w_w[:].bitcast(I32), in_=w_words[0].bitcast(I32))
        nc.sync.dma_start(out=list4[:], in_=offs4)
        nc.sync.dma_start(out=list3[:], in_=offs3)
        for h in range(N // P):
            nc.sync.dma_start(out=tz_t[h][:], in_=tz[h * P : (h + 1) * P, :])
        nc.sync.dma_start(out=list5[:], in_=offs5)
        nc.sync.dma_start(out=wb_w[:].bitcast(I32), in_=wb_words[0].rearrange("p c b -> p (c b)").bitcast(I32))
        load_scale_rows(wb_s, wb_scales)

        def deal_columns(copy, dealt, src, element_bytes):
            run = LINE_BYTES // element_bytes
            copy(
                out=dealt[:].rearrange("p t (c i) -> p c t i", i=run),
                in_=src[:].rearrange("p (c i t) -> p c t i", i=run, t=PACK),
            )

        x1_pair = [tile("x1_pair%d" % u, [P, 2, J], BF16) for u in range(2)]
        x1_woven = [tile("x1_woven%d" % s, [P, P, PACK], BF16) for s in range(2)]
        x1_codes = tile("x1_codes", [P, J], U32)
        x1_scales = tile("x1_scales", [P, J], U8)
        for u in range(2):
            for v in range(2):
                t = 2 * u + v
                nc.scalar.activation(
                    out=x1_pair[u][:, v, :], in_=cq_t[t][:].indirect(list1[:]), func=COPY, scale=ga_t[:, t : t + 1]
                )
            for s in range(2):
                nc.vector.tensor_copy(
                    out=x1_woven[s][:, :, 2 * u : 2 * u + 2],
                    in_=x1_pair[u][:, :, s * P : (s + 1) * P].rearrange("p v j -> p j v"),
                )
        for s in range(2):
            nc.vector.quantize_mx(
                out=x1_codes[:, s * P : (s + 1) * P].bitcast(E4M3), scales=x1_scales[:, s * P : (s + 1) * P],
                in_=x1_woven[s][:].rearrange("p j t -> p (j t)"),
            )

        w_dealt = tile("w_dealt", [P, PACK, P], U16)
        w_s_dealt = tile("w_s_dealt", [P, PACK, P], U8)
        deal_columns(nc.scalar.copy, w_dealt, w_w, 2)
        deal_columns(nc.vector.tensor_copy, w_s_dealt, w_s, 1)
        a_t = [tile("a%d" % t, [P, J], F32) for t in range(PACK)]
        for t in range(PACK):
            width = P if t == 0 else J
            for start in range(0, J, width):
                slots = slice(start, start + width)
                a_bank = banks.tile([P, width], F32, name="a_bank%d_%d" % (t, start))
                nc.tensor.matmul_mx(
                    out=a_bank[:], lhsT=w_dealt[:, t, :].bitcast(E2M1), lhsT_scale=w_s_dealt[:, t, :],
                    rhs=x1_codes[:, slots].bitcast(E4M3), rhs_scale=x1_scales[:, slots], start=True, stop=True,
                )
                nc.vector.tensor_copy(out=a_t[t][:, slots], in_=a_bank[:])

        xo_w_picked = tile("xo_w_picked", [P, J], U16)
        xo_s_picked = tile("xo_s_picked", [P, J], U8)
        nc.vector.tensor_copy(out=xo_w_picked[:], in_=xo_w[:].indirect(list2[:]))
        spread_scale_rows(xo_s, xo_stage, 0)
        nc.vector.tensor_copy(out=xo_s_picked[:], in_=xo_s[:].indirect(list2[:]))
        spread_scale_rows(w2_s, w2_stage, HALF)
        w2_dealt = tile("w2_dealt", [P, PACK, P], U32)
        w2_s_dealt = tile("w2_s_dealt", [P, PACK, P], U8)
        deal_columns(nc.scalar.copy, w2_dealt, w2_w, 4)
        deal_columns(nc.vector.tensor_copy, w2_s_dealt, w2_s, 1)
        b_bank = [banks.tile([P, 2, J], F32, name="b_bank%d" % u, tag="b_then_p%d" % u) for u in range(2)]
        b_t = [tile("b%d" % t, [P, J], F32) for t in range(PACK)]
        b_picked = [tile("b_picked%d" % u, [P, 2, O], F32) for u in range(2)]
        for u in range(2):
            for v in range(2):
                t = 2 * u + v
                nc.tensor.matmul_mx(
                    out=b_bank[u][:, v, :], lhsT=w2_dealt[:, t, :].bitcast(E5M2), lhsT_scale=w2_s_dealt[:, t, :],
                    rhs=xo_w_picked[:].bitcast(E2M1), rhs_scale=xo_s_picked[:], start=True, stop=True,
                )
            for v in range(2):
                nc.vector.tensor_copy(out=b_t[2 * u + v][:], in_=b_bank[u][:, v, :])
        for t in range(PACK):
            nc.scalar.activation(
                out=b_picked[t // 2][:, t % 2, :], in_=b_t[t][:].indirect(list4[:]), func=COPY, scale=sb_t[:, t : t + 1]
            )

        a_picked = [tile("a_picked%d" % u, [P, 2, O], F32) for u in range(2)]
        hid_woven = tile("hid_woven", [P, O, PACK], BF16)
        hid_codes = tile("hid_codes", [P, O], U32)
        hid_scales = tile("hid_scales", [P, O], U8)
        for u in range(2):
            for v in range(2):
                t = 2 * u + v
                nc.scalar.activation(
                    out=a_picked[u][:, v, :], in_=a_t[t][:].indirect(list3[:]), func=COPY, scale=sa_t[:, t : t + 1]
                )
            nc.vector.tensor_tensor(
                out=hid_woven[:, :, 2 * u : 2 * u + 2], in0=a_picked[u][:].rearrange("p v o -> p o v"),
                in1=b_picked[u][:].rearrange("p v o -> p o v"), op=MAX,
            )
        nc.vector.quantize_mx(
            out=hid_codes[:].bitcast(E4M3), scales=hid_scales[:], in_=hid_woven[:].rearrange("p o t -> p (o t)")
        )

        for h in range(N // P):
            features = slice(h * P, (h + 1) * P)
            floor_t = tile("floor%d" % h, [P, O], F32)
            y_t = tile("y%d" % h, [P, O], F32)
            p_bank = banks.tile([P, O], F32, name="p_bank%d" % h, tag="b_then_p%d" % h)
            nc.scalar.activation(out=floor_t[:], in_=tz_t[h][:].indirect(list5[:]), func=COPY, scale=so_t[:, h : h + 1])
            nc.tensor.matmul_mx(
                out=p_bank[:], lhsT=wb_w[:, features].bitcast(E5M2), lhsT_scale=wb_s[:, features],
                rhs=hid_codes[:].bitcast(E4M3), rhs_scale=hid_scales[:], start=True, stop=True,
            )
            nc.vector.tensor_tensor(out=y_t[:], in0=p_bank[:], in1=floor_t[:], op=MAX)
            nc.sync.dma_start(out=out[features, :], in_=y_t[:])
